import numpy as np
import ml_dtypes


def mxq(x, axis, fmt="e4m3"):
    dtype, down = {"e4m3": (ml_dtypes.float8_e4m3fn, 7), "e5m2": (ml_dtypes.float8_e5m2, 14)}[fmt]
    v = np.moveaxis(np.asarray(x, np.float32).astype(ml_dtypes.bfloat16).astype(np.float64), axis, -1)
    blocks = v.reshape(v.shape[:-1] + (-1, 32))
    amax = np.abs(blocks).max(-1, keepdims=True)
    byte = np.maximum(np.where(amax > 0, np.frexp(amax)[1] - 1 + 127, 0) - down, 1)
    scale = np.exp2(byte - 127.0)
    codes = (blocks / scale).astype(np.float32).astype(dtype).astype(np.float64)
    return np.moveaxis((codes * scale).reshape(v.shape), -1, axis)


WIDE = False


def mx_kscale(k):
    if not WIDE:
        return np.ones(k)
    levels = np.array([10, -10, 5, -5, 0])
    if k % 512:
        return np.exp2(np.random.permutation(np.resize(levels, k // 32))).repeat(32)
    a = np.empty((k // 512, 16))
    for p in range(k // 512):
        a[p, :8] = np.random.permutation(np.resize(levels, 8))
        for g in range(8):
            far = levels[np.abs(levels - a[p, g]) >= 10]
            a[p, g + 8] = far[np.random.randint(len(far))]
    return np.exp2(a.ravel()).repeat(32)


def f64(x):
    return np.asarray(x).astype(np.float64)


def striped(idx):
    return np.tile(idx.reshape(-1, 16).T, (8, 1)).astype(np.uint16)


def unstriped(offs):
    return offs[:16].T.reshape(-1).astype(np.int64)


def striped8(idx):
    return np.concatenate([x.reshape(-1, 16).T for x in idx]).astype(np.uint16)


def runs(offs, k):
    lists = np.stack([offs[16 * r : 16 * r + 16].T.reshape(-1) for r in range(8)]).astype(np.int64)
    return lists[np.arange(k) % 512 // 64]


def pack_weight(w):
    k, n = w.shape
    w = f64(np.asarray(w, np.float32).astype(ml_dtypes.bfloat16)).reshape(k // 32, 32, n)
    amax = np.abs(w).max(1)
    byte = np.clip(np.where(amax > 0, np.frexp(amax)[1] - 1 + 127 - 7, 1), 1, 254)
    scaled = (w * np.exp2(127.0 - byte)[:, None, :]).reshape(k, n).astype(np.float32)
    words = np.ascontiguousarray(scaled.reshape(k // 512, 128, 4, n).transpose(0, 1, 3, 2)).astype(ml_dtypes.float8_e4m3fn).view(np.uint8)
    return words, np.ascontiguousarray(byte.astype(np.uint8).reshape(k // 512, 16, n))


def unpack_weight(words, scales):
    g, p, n, _ = words.shape
    vals = np.ascontiguousarray(words).view(ml_dtypes.float8_e4m3fn).astype(np.float64) * np.repeat(np.exp2(scales.astype(np.float64) - 127.0), 8, axis=1)[..., None]
    return vals.transpose(0, 1, 3, 2).reshape(g * 512, n)


def relu(v):
    return np.maximum(v, 0.0)

def planes(y):
    n, m = y.shape
    v = y.astype(np.float32).astype(ml_dtypes.bfloat16).astype(np.float64).reshape(n // 32, 32, m)
    top = np.abs(v).max(1)
    byte = np.clip(np.where(top > 0, np.frexp(top)[1] - 1 + 127 - 7, 1), 1, 254)
    codes = (v * np.exp2(127.0 - byte)[:, None, :]).reshape(n, m).astype(np.float32).astype(ml_dtypes.float8_e4m3fn).view(np.uint8)
    words = codes.reshape(n // 512, 128, 4, m).transpose(0, 1, 3, 2)
    return np.ascontiguousarray(words), np.ascontiguousarray(byte.astype(np.uint8).reshape(n // 512, 16, m))


K, T, S, N, G, H = 512, 2048, 512, 512, 2048, 512


def setup_inputs():
    n = np.random.standard_normal
    s = mx_kscale(K)[:, None]
    u = mx_kscale(H)
    packed_xT = pack_weight(n((K, T)) * s)
    packed_dT = pack_weight(n((K, G)) / s)
    packed_w1 = pack_weight(n((H, N)) / np.sqrt(H) / u[:, None])
    return {
        "x_words": packed_xT[0],
        "x_scales": packed_xT[1],
        "d_words": packed_dT[0],
        "d_scales": packed_dT[1],
        "gn": (np.random.uniform(0.5, 1.5, (H, 1)) * u[:, None]).astype(np.float32),
        "w1_words": packed_w1[0],
        "w1_scales": packed_w1[1],
        "offs": striped(np.random.permutation(T)[:S]),
        "k1": striped8(np.random.randint(0, G, (8, H))),
        "k2": striped8(np.random.randint(0, G, (8, H))),
    }


def reference(x_words, x_scales, d_words, d_scales, gn, w1_words, w1_scales, offs, k1, k2):
    d_k2 = unpack_weight(d_words, d_scales)[np.arange(K)[:, None], runs(k2, K)]
    xq = unpack_weight(x_words, x_scales)[:, unstriped(offs)]
    d_k1 = unpack_weight(d_words, d_scales)[np.arange(K)[:, None], runs(k1, K)]
    h = relu(0.0625 * (d_k1.T @ xq))
    z = f64(gn) * h
    hw = unpack_weight(w1_words, w1_scales).T @ mxq(z, 0, "e4m3")
    out_0 = 0.0625 * (d_k2.T @ xq) + hw
    return (out_0,) + planes(out_0)

@@ -1,0 +1,239 @@
+from contextlib import ExitStack
+
+import concourse.mybir as mybir
+
+K, T, S, N, G, H = 512, 2048, 512, 512, 2048, 512
+FLOPS = 3 * 2 * 512 * 512 * 512
+
+F32 = mybir.dt.float32
+BF16 = mybir.dt.bfloat16
+I32 = mybir.dt.int32
+U32 = mybir.dt.uint32
+U16 = mybir.dt.uint16
+U8 = mybir.dt.uint8
+FP8X4 = mybir.dt.float8_e4m3fn_x4
+ALU = mybir.AluOpType
+COPY = mybir.ActivationFunctionType.Copy
+
+P = 128
+PACK = 4
+CHUNK = 128
+CHUNKS = S // CHUNK
+HALF = S // 2
+SCALAR_ROUNDS = 1
+
+
+def words_of(dram):
+    return dram[0].rearrange("p n t -> p (n t)").bitcast(I32)
+
+
+def deal_words(nc, dealt, plain):
+    nc.vector.tensor_copy(
+        out=dealt.rearrange("p (t c i) -> p c t i", t=PACK, i=PACK),
+        in_=plain.rearrange("p (c i t) -> p c t i", t=PACK, i=PACK),
+    )
+
+
+def deal_bytes(nc, dealt, plain):
+    nc.vector.tensor_copy(
+        out=dealt.rearrange("p (t m) -> p t m", t=PACK),
+        in_=plain.rearrange("p (m t) -> p t m", t=PACK),
+    )
+
+
+def tile_picked_pqskip_relu_po_kernel(
+    tc, x_words, x_scales, d_words, d_scales, gn, w1_words, w1_scales, offs, k1, k2, out_0, out_1, out_2
+):
+    nc = tc.nc
+    with ExitStack() as ctx:
+        sb = ctx.enter_context(tc.tile_pool(name="sb", bufs=1))
+        ps = ctx.enter_context(tc.psum_pool(name="ps", bufs=1))
+
+        def tile(name, cols, dtype, after=None):
+            return sb.tile([P, cols], dtype, name=name, tag=after or name, align_bytes=64)
+
+        k1_list = sb.tile([P, H // 16], U16, name="k1_list")
+        k2_list = sb.tile([P, N // 16], U16, name="k2_list")
+        offs_list = sb.tile([P, S // 16], U16, name="offs_list")
+        d_word_table = tile("d_word_table", G, U32)
+        x_word_table = tile("x_word_table", T, U32)
+        d_byte_table = tile("d_byte_table", G, U8)
+        x_byte_table = tile("x_byte_table", T, U8)
+        w1_word_plain = tile("w1_word_plain", N, U32)
+        w1_byte_plain = tile("w1_byte_plain", N, U8)
+        gain = tile("gain", PACK, F32)
+
+        for table in (d_byte_table, x_byte_table, w1_byte_plain):
+            nc.vector.memset(table[:].bitcast(I32), 0)
+
+        warm_in = tile("warm_in", 1, F32)
+        warm_out = tile("warm_out", 1, F32)
+        nc.vector.memset(warm_in[:], 0.0)
+        nc.scalar.activation(out=warm_out[:], in_=warm_in[:], func=COPY, scale=0.0625)
+
+        d_rows = d_scales[0].bitcast(I32)
+        x_rows = x_scales[0].bitcast(I32)
+        w1_rows = w1_scales[0].bitcast(I32)
+        nc.sync.dma_start(k1_list[:], k1)
+        nc.sync.dma_start(k2_list[:], k2)
+        for e in range(2):
+            nc.sync.dma_start(d_byte_table[e:P:16, :].bitcast(I32), d_rows[e:16:2, :])
+        nc.sync.dma_start(x_word_table[:].bitcast(I32), words_of(x_words))
+        nc.sync.dma_start(offs_list[:], offs)
+        for i in range(4):
+            nc.scalar.dma_start(x_byte_table[i:P:32, :].bitcast(I32), x_rows[i:16:4, :])
+        nc.sync.dma_start(d_word_table[:].bitcast(I32), words_of(d_words))
+        for i in range(4):
+            nc.sync.dma_start(w1_byte_plain[i:P:32, :].bitcast(I32), w1_rows[i:16:4, :])
+        nc.sync.dma_start(gain[:], gn.rearrange("(p t) o -> p (t o)", t=PACK))
+        nc.sync.dma_start(w1_word_plain[:].bitcast(I32), words_of(w1_words))
+
+        byte_picked = tile("byte_picked", H + N, U8)
+        coded_bytes = tile("coded_bytes", H + N, U8)
+        nc.vector.tensor_copy(byte_picked[:, :H], d_byte_table[:].indirect(k1_list[:]))
+        nc.vector.tensor_copy(byte_picked[:, H:], d_byte_table[:].indirect(k2_list[:]))
+        deal_bytes(nc, coded_bytes[:, :H], byte_picked[:, :H])
+        deal_bytes(nc, coded_bytes[:, H:], byte_picked[:, H:])
+        for e in range(2):
+            nc.scalar.dma_start(coded_bytes[2 + e : P : 32, :].bitcast(I32), coded_bytes[16 + e : P : 32, :].bitcast(I32))
+        k1_bytes = coded_bytes[:, :H]
+        k2_bytes = coded_bytes[:, H:]
+
+        x_bytes = tile("x_bytes", S, U8)
+        x_wds = tile("x_wds", S, U32)
+        nc.vector.tensor_copy(x_bytes[:], x_byte_table[:].indirect(offs_list[:]))
+        nc.vector.tensor_copy(x_wds[:], x_word_table[:].indirect(offs_list[:]))
+
+        k1_picked = tile("k1_picked", H, U32)
+        k2_picked = [tile("k2_picked0", N // 2, U32), None]
+        k1_words = tile("k1_words", H, U32)
+        k2_words = tile("k2_words", N, U32)
+        nc.vector.tensor_copy(k1_picked[:], d_word_table[:].indirect(k1_list[:]))
+        nc.vector.tensor_copy(k2_picked[0][:], d_word_table[:].indirect(k2_list[:, : N // 32]))
+        deal_words(nc, k1_words[:], k1_picked[:])
+        k2_picked[1] = tile("k2_picked1", N // 2, U32, "k1_picked")
+        nc.vector.tensor_copy(k2_picked[1][:], d_word_table[:].indirect(k2_list[:, N // 32 :]))
+
+        def tokens(c):
+            cols = slice(c * CHUNK, (c + 1) * CHUNK)
+            return x_wds[:, cols].bitcast(FP8X4), x_bytes[:, cols]
+
+        hidden = []
+        for c in range(CHUNKS):
+            bank = ps.tile([P, PACK * CHUNK], F32, name="hidden%d" % c)
+            rhs, rhs_scale = tokens(c)
+            for t in range(PACK):
+                cols = slice(t * P, (t + 1) * P)
+                nc.tensor.matmul_mx(
+                    out=bank[:, cols], lhsT=k1_words[:, cols].bitcast(FP8X4), lhsT_scale=k1_bytes[:, cols],
+                    rhs=rhs, rhs_scale=rhs_scale, start=True, stop=True,
+                )
+            hidden.append(bank)
+
+        for half in range(2):
+            nc.vector.tensor_copy(
+                out=k2_words[:].rearrange("p (t h c i) -> p h c t i", t=PACK, h=2, i=PACK)[:, half],
+                in_=k2_picked[half][:].rearrange("p (c i t) -> p c t i", t=PACK, i=PACK),
+            )
+        w1_wds = tile("w1_wds", N, U32)
+        w1_bytes = tile("w1_bytes", N, U8)
+        deal_words(nc, w1_wds[:], w1_word_plain[:])
+        deal_bytes(nc, w1_bytes[:], w1_byte_plain[:])
+
+        z_rounded = [tile("z_rounded%d" % c, PACK * CHUNK, BF16) for c in range(CHUNKS)]
+        z_words = [tile("z_words%d" % c, CHUNK, U32) for c in range(CHUNKS)]
+        z_bytes = [tile("z_bytes%d" % c, CHUNK, U8) for c in range(CHUNKS)]
+        y = [tile("y%d" % c, PACK * CHUNK, F32) for c in range(CHUNKS)]
+        y_rounded = [tile("y_rounded%d" % c, PACK * CHUNK, BF16) for c in range(CHUNKS)]
+        y_words = [tile("y_words%d" % c, CHUNK, U32) for c in range(CHUNKS)]
+        y_bytes = tile("y_bytes", S, U8)
+
+        def make_z(c):
+            nc.vector.scalar_tensor_tensor(
+                out=z_rounded[c][:].rearrange("p (j t) -> p j t", t=PACK),
+                in0=hidden[c][:].rearrange("p (t j) -> p j t", t=PACK),
+                scalar=0.0,
+                in1=gain[:].unsqueeze(1).to_broadcast([P, CHUNK, PACK]),
+                op0=ALU.max,
+                op1=ALU.mult,
+            )
+
+        def quantize_z(c):
+            nc.vector.quantize_mx(out=z_words[c][:].bitcast(FP8X4), scales=z_bytes[c][:], in_=z_rounded[c][:])
+
+        def shortcut(c, t, target):
+            cols = slice(t * P, (t + 1) * P)
+            rhs, rhs_scale = tokens(c)
+            nc.tensor.matmul_mx(
+                out=target, lhsT=k2_words[:, cols].bitcast(FP8X4), lhsT_scale=k2_bytes[:, cols],
+                rhs=rhs, rhs_scale=rhs_scale, start=True, stop=False,
+            )
+
+        def dense(c, t, target):
+            cols = slice(t * P, (t + 1) * P)
+            nc.tensor.matmul_mx(
+                out=target, lhsT=w1_wds[:, cols].bitcast(FP8X4), lhsT_scale=w1_bytes[:, cols],
+                rhs=z_words[c][:].bitcast(FP8X4), rhs_scale=z_bytes[c][:], start=False, stop=True,
+            )
+
+        def store_y(c):
+            nc.sync.dma_start(
+                out_0.rearrange("(p t) j -> p t j", t=PACK)[:, :, c * CHUNK : (c + 1) * CHUNK],
+                y[c][:].rearrange("p (t j) -> p t j", t=PACK),
+            )
+
+        def second_layer(c):
+            bank = ps.tile([P, PACK * CHUNK], F32, name="result%d" % c)
+            for t in range(PACK):
+                target = bank[:, t * CHUNK : (t + 1) * CHUNK]
+                shortcut(c, t, target)
+                dense(c, t, target)
+            woven = y_rounded[c][:].rearrange("p (j t) -> p j t", t=PACK)
+            if c < SCALAR_ROUNDS:
+                nc.scalar.activation(out=woven, in_=bank[:].rearrange("p (t j) -> p j t", t=PACK), func=COPY, scale=0.0625)
+            nc.scalar.activation(out=y[c][:], in_=bank[:], func=COPY, scale=0.0625)
+            store_y(c)
+
+        def last_shortcut():
+            c = CHUNKS - 1
+            tags = ["spare"] + ["hidden%d" % i for i in range(PACK - 1)]
+            banks = [ps.tile([P, PACK * CHUNK], F32, name="last%d" % t, tag=tags[t]) for t in range(PACK)]
+            for t in range(PACK):
+                shortcut(c, t, banks[t][:, :CHUNK])
+            return banks
+
+        def last_dense(banks):
+            c = CHUNKS - 1
+            for t in range(PACK):
+                dense(c, t, banks[t][:, :CHUNK])
+                part = y[c][:, t * CHUNK : (t + 1) * CHUNK]
+                if t % 2:
+                    nc.vector.tensor_scalar_mul(part, banks[t][:, :CHUNK], 0.0625)
+                else:
+                    nc.scalar.activation(out=part, in_=banks[t][:, :CHUNK], func=COPY, scale=0.0625)
+            store_y(c)
+
+        def quantize_y(c):
+            cols = slice(c * CHUNK, (c + 1) * CHUNK)
+            if c >= SCALAR_ROUNDS:
+                nc.vector.tensor_copy(
+                    out=y_rounded[c][:].rearrange("p (a i t) -> p a t i", t=PACK, i=PACK),
+                    in_=y[c][:].rearrange("p (t a i) -> p a t i", t=PACK, i=PACK),
+                )
+            nc.vector.quantize_mx(out=y_words[c][:].bitcast(FP8X4), scales=y_bytes[:, cols], in_=y_rounded[c][:])
+            nc.sync.dma_start(words_of(out_1)[:, cols], y_words[c][:].bitcast(I32))
+
+        make_z(0)
+        for c in range(1, CHUNKS):
+            make_z(c)
+            quantize_z(c - 1)
+            second_layer(c - 1)
+        banks = last_shortcut()
+        quantize_z(CHUNKS - 1)
+        last_dense(banks)
+        for c in range(CHUNKS):
+            quantize_y(c)
+        y_rows = out_2[0].bitcast(I32)
+        for i in range(4):
+            queue = nc.sync if i % 2 else nc.scalar
+            queue.dma_start(y_rows[i:16:4, :], y_bytes[i:P:32, :].bitcast(I32))

@@ -20,22 +20,22 @@ PACK = 4
 CHUNK = 128
 CHUNKS = S // CHUNK
 HALF = S // 2
-SCALAR_ROUNDS = 1
+WARM_PASSES = 3
 
 
 def words_of(dram):
     return dram[0].rearrange("p n t -> p (n t)").bitcast(I32)
 
 
-def deal_words(nc, dealt, plain):
-    nc.vector.tensor_copy(
+def deal_words(engine, dealt, plain):
+    engine.tensor_copy(
         out=dealt.rearrange("p (t c i) -> p c t i", t=PACK, i=PACK),
         in_=plain.rearrange("p (c i t) -> p c t i", t=PACK, i=PACK),
     )
 
 
-def deal_bytes(nc, dealt, plain):
-    nc.vector.tensor_copy(
+def deal_bytes(engine, dealt, plain):
+    engine.tensor_copy(
         out=dealt.rearrange("p (t m) -> p t m", t=PACK),
         in_=plain.rearrange("p (m t) -> p t m", t=PACK),
     )
@@ -63,60 +63,65 @@ def tile_picked_pqskip_relu_po_kernel(
         w1_byte_plain = tile("w1_byte_plain", N, U8)
         gain = tile("gain", PACK, F32)
 
-        for table in (d_byte_table, x_byte_table, w1_byte_plain):
+        for table in (d_byte_table, w1_byte_plain, x_byte_table):
             nc.vector.memset(table[:].bitcast(I32), 0)
-
-        warm_in = tile("warm_in", 1, F32)
-        warm_out = tile("warm_out", 1, F32)
-        nc.vector.memset(warm_in[:], 0.0)
-        nc.scalar.activation(out=warm_out[:], in_=warm_in[:], func=COPY, scale=0.0625)
 
         d_rows = d_scales[0].bitcast(I32)
         x_rows = x_scales[0].bitcast(I32)
         w1_rows = w1_scales[0].bitcast(I32)
         nc.sync.dma_start(k1_list[:], k1)
         nc.sync.dma_start(k2_list[:], k2)
-        for e in range(2):
-            nc.sync.dma_start(d_byte_table[e:P:16, :].bitcast(I32), d_rows[e:16:2, :])
-        nc.sync.dma_start(x_word_table[:].bitcast(I32), words_of(x_words))
         nc.sync.dma_start(offs_list[:], offs)
-        for i in range(4):
-            nc.scalar.dma_start(x_byte_table[i:P:32, :].bitcast(I32), x_rows[i:16:4, :])
+        for table, rows in ((d_byte_table, d_rows), (w1_byte_plain, w1_rows)):
+            for e in range(2):
+                nc.sync.dma_start(table[e:P:16, :].bitcast(I32), rows[e:16:2, :])
         nc.sync.dma_start(d_word_table[:].bitcast(I32), words_of(d_words))
         for i in range(4):
-            nc.sync.dma_start(w1_byte_plain[i:P:32, :].bitcast(I32), w1_rows[i:16:4, :])
+            nc.sync.dma_start(x_byte_table[i:P:32, :].bitcast(I32), x_rows[i:16:4, :])
+        nc.sync.dma_start(x_word_table[:].bitcast(I32), words_of(x_words))
         nc.sync.dma_start(gain[:], gn.rearrange("(p t) o -> p (t o)", t=PACK))
         nc.sync.dma_start(w1_word_plain[:].bitcast(I32), words_of(w1_words))
 
         byte_picked = tile("byte_picked", H + N, U8)
-        coded_bytes = tile("coded_bytes", H + N, U8)
+        dealt_bytes = tile("dealt_bytes", H + 2 * N, U8)
+        k1_bytes = dealt_bytes[:, :H]
+        k2_bytes = dealt_bytes[:, H : H + N]
+        w1_bytes = dealt_bytes[:, H + N :]
         nc.vector.tensor_copy(byte_picked[:, :H], d_byte_table[:].indirect(k1_list[:]))
         nc.vector.tensor_copy(byte_picked[:, H:], d_byte_table[:].indirect(k2_list[:]))
-        deal_bytes(nc, coded_bytes[:, :H], byte_picked[:, :H])
-        deal_bytes(nc, coded_bytes[:, H:], byte_picked[:, H:])
+        deal_bytes(nc.vector, k1_bytes, byte_picked[:, :H])
+        deal_bytes(nc.vector, k2_bytes, byte_picked[:, H:])
+        deal_bytes(nc.gpsimd, w1_bytes, w1_byte_plain[:])
         for e in range(2):
-            nc.scalar.dma_start(coded_bytes[2 + e : P : 32, :].bitcast(I32), coded_bytes[16 + e : P : 32, :].bitcast(I32))
-        k1_bytes = coded_bytes[:, :H]
-        k2_bytes = coded_bytes[:, H:]
+            nc.scalar.dma_start(dealt_bytes[2 + e : P : 32, :].bitcast(I32), dealt_bytes[16 + e : P : 32, :].bitcast(I32))
 
-        x_bytes = tile("x_bytes", S, U8)
-        x_wds = tile("x_wds", S, U32)
-        nc.vector.tensor_copy(x_bytes[:], x_byte_table[:].indirect(offs_list[:]))
-        nc.vector.tensor_copy(x_wds[:], x_word_table[:].indirect(offs_list[:]))
+        def pick_half(out, table, lists, half):
+            cols = slice(half * HALF // 16, (half + 1) * HALF // 16)
+            nc.vector.tensor_copy(out[:], table[:].indirect(lists[:, cols]))
+            return out
 
         k1_picked = tile("k1_picked", H, U32)
-        k2_picked = [tile("k2_picked0", N // 2, U32), None]
         k1_words = tile("k1_words", H, U32)
-        k2_words = tile("k2_words", N, U32)
+        x_bytes = tile("x_bytes", S, U8)
         nc.vector.tensor_copy(k1_picked[:], d_word_table[:].indirect(k1_list[:]))
-        nc.vector.tensor_copy(k2_picked[0][:], d_word_table[:].indirect(k2_list[:, : N // 32]))
-        deal_words(nc, k1_words[:], k1_picked[:])
-        k2_picked[1] = tile("k2_picked1", N // 2, U32, "k1_picked")
-        nc.vector.tensor_copy(k2_picked[1][:], d_word_table[:].indirect(k2_list[:, N // 32 :]))
+        k2_picked = tile("k2_picked", N, U32)
+        nc.vector.tensor_copy(k2_picked[:], d_word_table[:].indirect(k2_list[:]))
+        deal_words(nc.vector, k1_words[:], k1_picked[:])
+        nc.vector.tensor_copy(x_bytes[:], x_byte_table[:].indirect(offs_list[:]))
+        x_wds = [pick_half(tile("x_wds%d" % half, HALF, U32), x_word_table, offs_list, half) for half in range(2)]
+        k2_words = tile("k2_words", N, U32, "x_word_table")
+        deal_words(nc.vector, k2_words[:], k2_picked[:])
 
         def tokens(c):
-            cols = slice(c * CHUNK, (c + 1) * CHUNK)
-            return x_wds[:, cols].bitcast(FP8X4), x_bytes[:, cols]
+            half, place = divmod(c * CHUNK, HALF)
+            return x_wds[half][:, place : place + CHUNK].bitcast(FP8X4), x_bytes[:, c * CHUNK : (c + 1) * CHUNK]
+
+        warm_bank = ps.tile([P, S], F32, name="warm_bank", tag="spare")
+        for i in range(WARM_PASSES):
+            nc.tensor.matmul_mx(
+                out=warm_bank[:], lhsT=k1_picked[:, :P].bitcast(FP8X4), lhsT_scale=k1_bytes[:, :P],
+                rhs=k1_picked[:].bitcast(FP8X4), rhs_scale=k1_bytes, start=True, stop=True,
+            )
 
         hidden = []
         for c in range(CHUNKS):
@@ -130,22 +135,10 @@ def tile_picked_pqskip_relu_po_kernel(
                 )
             hidden.append(bank)
 
-        for half in range(2):
-            nc.vector.tensor_copy(
-                out=k2_words[:].rearrange("p (t h c i) -> p h c t i", t=PACK, h=2, i=PACK)[:, half],
-                in_=k2_picked[half][:].rearrange("p (c i t) -> p c t i", t=PACK, i=PACK),
-            )
-        w1_wds = tile("w1_wds", N, U32)
-        w1_bytes = tile("w1_bytes", N, U8)
-        deal_words(nc, w1_wds[:], w1_word_plain[:])
-        deal_bytes(nc, w1_bytes[:], w1_byte_plain[:])
-
         z_rounded = [tile("z_rounded%d" % c, PACK * CHUNK, BF16) for c in range(CHUNKS)]
         z_words = [tile("z_words%d" % c, CHUNK, U32) for c in range(CHUNKS)]
         z_bytes = [tile("z_bytes%d" % c, CHUNK, U8) for c in range(CHUNKS)]
         y = [tile("y%d" % c, PACK * CHUNK, F32) for c in range(CHUNKS)]
-        y_rounded = [tile("y_rounded%d" % c, PACK * CHUNK, BF16) for c in range(CHUNKS)]
-        y_words = [tile("y_words%d" % c, CHUNK, U32) for c in range(CHUNKS)]
         y_bytes = tile("y_bytes", S, U8)
 
         def make_z(c):
@@ -157,6 +150,10 @@ def tile_picked_pqskip_relu_po_kernel(
                 op0=ALU.max,
                 op1=ALU.mult,
             )
+
+        make_z(0)
+        w1_wds = tile("w1_wds", N, U32)
+        deal_words(nc.gpsimd, w1_wds[:], w1_word_plain[:])
 
         def quantize_z(c):
             nc.vector.quantize_mx(out=z_words[c][:].bitcast(FP8X4), scales=z_bytes[c][:], in_=z_rounded[c][:])
@@ -188,9 +185,6 @@ def tile_picked_pqskip_relu_po_kernel(
                 target = bank[:, t * CHUNK : (t + 1) * CHUNK]
                 shortcut(c, t, target)
                 dense(c, t, target)
-            woven = y_rounded[c][:].rearrange("p (j t) -> p j t", t=PACK)
-            if c < SCALAR_ROUNDS:
-                nc.scalar.activation(out=woven, in_=bank[:].rearrange("p (t j) -> p j t", t=PACK), func=COPY, scale=0.0625)
             nc.scalar.activation(out=y[c][:], in_=bank[:], func=COPY, scale=0.0625)
             store_y(c)
 
@@ -213,17 +207,25 @@ def tile_picked_pqskip_relu_po_kernel(
                     nc.scalar.activation(out=part, in_=banks[t][:, :CHUNK], func=COPY, scale=0.0625)
             store_y(c)
 
-        def quantize_y(c):
-            cols = slice(c * CHUNK, (c + 1) * CHUNK)
-            if c >= SCALAR_ROUNDS:
-                nc.vector.tensor_copy(
-                    out=y_rounded[c][:].rearrange("p (a i t) -> p a t i", t=PACK, i=PACK),
-                    in_=y[c][:].rearrange("p (t a i) -> p a t i", t=PACK, i=PACK),
-                )
-            nc.vector.quantize_mx(out=y_words[c][:].bitcast(FP8X4), scales=y_bytes[:, cols], in_=y_rounded[c][:])
-            nc.sync.dma_start(words_of(out_1)[:, cols], y_words[c][:].bitcast(I32))
+        def quantize_y(half):
+            rounded = tile("y_rounded%d" % half, PACK * HALF, BF16, "z_rounded%d" % (CHUNKS - 1 - half))
+            for c in range(2 * half, 2 * half + 2):
+                part = rounded[:, (c % 2) * PACK * CHUNK : (c % 2 + 1) * PACK * CHUNK]
+                if c == CHUNKS - 2:
+                    nc.scalar.copy(
+                        out=part.rearrange("p (j t) -> p j t", t=PACK),
+                        in_=y[c][:].rearrange("p (t j) -> p j t", t=PACK),
+                    )
+                else:
+                    nc.vector.tensor_copy(
+                        out=part.rearrange("p (a i t) -> p a t i", t=PACK, i=PACK),
+                        in_=y[c][:].rearrange("p (t a i) -> p a t i", t=PACK, i=PACK),
+                    )
+            y_words = tile("y_words%d" % half, HALF, U32, "z_words%d" % (CHUNKS - 1 - half))
+            cols = slice(half * HALF, (half + 1) * HALF)
+            nc.vector.quantize_mx(out=y_words[:].bitcast(FP8X4), scales=y_bytes[:, cols], in_=rounded[:])
+            nc.sync.dma_start(words_of(out_1)[:, cols], y_words[:].bitcast(I32))
 
-        make_z(0)
         for c in range(1, CHUNKS):
             make_z(c)
             quantize_z(c - 1)
@@ -231,8 +233,8 @@ def tile_picked_pqskip_relu_po_kernel(
         banks = last_shortcut()
         quantize_z(CHUNKS - 1)
         last_dense(banks)
-        for c in range(CHUNKS):
-            quantize_y(c)
+        for half in range(2):
+            quantize_y(half)
         y_rows = out_2[0].bitcast(I32)
         for i in range(4):
             queue = nc.sync if i % 2 else nc.scalar

@@ -20,7 +20,6 @@ PACK = 4
 CHUNK = 128
 CHUNKS = S // CHUNK
 HALF = S // 2
-WARM_PASSES = 3
 
 
 def words_of(dram):
@@ -115,13 +114,6 @@ def tile_picked_pqskip_relu_po_kernel(
         def tokens(c):
             half, place = divmod(c * CHUNK, HALF)
             return x_wds[half][:, place : place + CHUNK].bitcast(FP8X4), x_bytes[:, c * CHUNK : (c + 1) * CHUNK]
-
-        warm_bank = ps.tile([P, S], F32, name="warm_bank", tag="spare")
-        for i in range(WARM_PASSES):
-            nc.tensor.matmul_mx(
-                out=warm_bank[:], lhsT=k1_picked[:, :P].bitcast(FP8X4), lhsT_scale=k1_bytes[:, :P],
-                rhs=k1_picked[:].bitcast(FP8X4), rhs_scale=k1_bytes, start=True, stop=True,
-            )
 
         hidden = []
         for c in range(CHUNKS):

from contextlib import ExitStack

import concourse.mybir as mybir

K, T, S, N, G, H = 512, 2048, 512, 512, 2048, 512
FLOPS = 3 * 2 * 512 * 512 * 512

F32 = mybir.dt.float32
BF16 = mybir.dt.bfloat16
I32 = mybir.dt.int32
U32 = mybir.dt.uint32
U16 = mybir.dt.uint16
U8 = mybir.dt.uint8
FP8X4 = mybir.dt.float8_e4m3fn_x4
ALU = mybir.AluOpType
COPY = mybir.ActivationFunctionType.Copy

P = 128
PACK = 4
CHUNK = 128
CHUNKS = S // CHUNK
HALF = S // 2


def words_of(dram):
    return dram[0].rearrange("p n t -> p (n t)").bitcast(I32)


def deal_words(engine, dealt, plain):
    engine.tensor_copy(
        out=dealt.rearrange("p (t c i) -> p c t i", t=PACK, i=PACK),
        in_=plain.rearrange("p (c i t) -> p c t i", t=PACK, i=PACK),
    )


def deal_bytes(engine, dealt, plain):
    engine.tensor_copy(
        out=dealt.rearrange("p (t m) -> p t m", t=PACK),
        in_=plain.rearrange("p (m t) -> p t m", t=PACK),
    )


def tile_picked_pqskip_relu_po_kernel(
    tc, x_words, x_scales, d_words, d_scales, gn, w1_words, w1_scales, offs, k1, k2, out_0, out_1, out_2
):
    nc = tc.nc
    with ExitStack() as ctx:
        sb = ctx.enter_context(tc.tile_pool(name="sb", bufs=1))
        ps = ctx.enter_context(tc.psum_pool(name="ps", bufs=1))

        def tile(name, cols, dtype, after=None):
            return sb.tile([P, cols], dtype, name=name, tag=after or name, align_bytes=64)

        k1_list = sb.tile([P, H // 16], U16, name="k1_list")
        k2_list = sb.tile([P, N // 16], U16, name="k2_list")
        offs_list = sb.tile([P, S // 16], U16, name="offs_list")
        d_word_table = tile("d_word_table", G, U32)
        x_word_table = tile("x_word_table", T, U32)
        d_byte_table = tile("d_byte_table", G, U8)
        x_byte_table = tile("x_byte_table", T, U8)
        w1_word_plain = tile("w1_word_plain", N, U32)
        w1_byte_plain = tile("w1_byte_plain", N, U8)
        gain = tile("gain", PACK, F32)

        for table in (d_byte_table, w1_byte_plain, x_byte_table):
            nc.vector.memset(table[:].bitcast(I32), 0)

        d_rows = d_scales[0].bitcast(I32)
        x_rows = x_scales[0].bitcast(I32)
        w1_rows = w1_scales[0].bitcast(I32)
        nc.sync.dma_start(k1_list[:], k1)
        nc.sync.dma_start(k2_list[:], k2)
        nc.sync.dma_start(offs_list[:], offs)
        for table, rows in ((d_byte_table, d_rows), (w1_byte_plain, w1_rows)):
            for e in range(2):
                nc.sync.dma_start(table[e:P:16, :].bitcast(I32), rows[e:16:2, :])
        nc.sync.dma_start(d_word_table[:].bitcast(I32), words_of(d_words))
        for i in range(4):
            nc.sync.dma_start(x_byte_table[i:P:32, :].bitcast(I32), x_rows[i:16:4, :])
        nc.sync.dma_start(x_word_table[:].bitcast(I32), words_of(x_words))
        nc.sync.dma_start(gain[:], gn.rearrange("(p t) o -> p (t o)", t=PACK))
        nc.sync.dma_start(w1_word_plain[:].bitcast(I32), words_of(w1_words))

        byte_picked = tile("byte_picked", H + N, U8)
        dealt_bytes = tile("dealt_bytes", H + 2 * N, U8)
        k1_bytes = dealt_bytes[:, :H]
        k2_bytes = dealt_bytes[:, H : H + N]
        w1_bytes = dealt_bytes[:, H + N :]
        nc.vector.tensor_copy(byte_picked[:, :H], d_byte_table[:].indirect(k1_list[:]))
        nc.vector.tensor_copy(byte_picked[:, H:], d_byte_table[:].indirect(k2_list[:]))
        deal_bytes(nc.vector, k1_bytes, byte_picked[:, :H])
        deal_bytes(nc.vector, k2_bytes, byte_picked[:, H:])
        deal_bytes(nc.gpsimd, w1_bytes, w1_byte_plain[:])
        for e in range(2):
            nc.scalar.dma_start(dealt_bytes[2 + e : P : 32, :].bitcast(I32), dealt_bytes[16 + e : P : 32, :].bitcast(I32))

        def pick_half(out, table, lists, half):
            cols = slice(half * HALF // 16, (half + 1) * HALF // 16)
            nc.vector.tensor_copy(out[:], table[:].indirect(lists[:, cols]))
            return out

        k1_picked = tile("k1_picked", H, U32)
        k1_words = tile("k1_words", H, U32)
        x_bytes = tile("x_bytes", S, U8)
        nc.vector.tensor_copy(k1_picked[:], d_word_table[:].indirect(k1_list[:]))
        k2_picked = tile("k2_picked", N, U32)
        nc.vector.tensor_copy(k2_picked[:], d_word_table[:].indirect(k2_list[:]))
        deal_words(nc.vector, k1_words[:], k1_picked[:])
        nc.vector.tensor_copy(x_bytes[:], x_byte_table[:].indirect(offs_list[:]))
        x_wds = [pick_half(tile("x_wds%d" % half, HALF, U32), x_word_table, offs_list, half) for half in range(2)]
        k2_words = tile("k2_words", N, U32, "x_word_table")
        deal_words(nc.vector, k2_words[:], k2_picked[:])

        def tokens(c):
            half, place = divmod(c * CHUNK, HALF)
            return x_wds[half][:, place : place + CHUNK].bitcast(FP8X4), x_bytes[:, c * CHUNK : (c + 1) * CHUNK]

        hidden = []
        for c in range(CHUNKS):
            bank = ps.tile([P, PACK * CHUNK], F32, name="hidden%d" % c)
            rhs, rhs_scale = tokens(c)
            for t in range(PACK):
                cols = slice(t * P, (t + 1) * P)
                nc.tensor.matmul_mx(
                    out=bank[:, cols], lhsT=k1_words[:, cols].bitcast(FP8X4), lhsT_scale=k1_bytes[:, cols],
                    rhs=rhs, rhs_scale=rhs_scale, start=True, stop=True,
                )
            hidden.append(bank)

        z_rounded = [tile("z_rounded%d" % c, PACK * CHUNK, BF16) for c in range(CHUNKS)]
        z_words = [tile("z_words%d" % c, CHUNK, U32) for c in range(CHUNKS)]
        z_bytes = [tile("z_bytes%d" % c, CHUNK, U8) for c in range(CHUNKS)]
        y = [tile("y%d" % c, PACK * CHUNK, F32) for c in range(CHUNKS)]
        y_bytes = tile("y_bytes", S, U8)

        def make_z(c):
            nc.vector.scalar_tensor_tensor(
                out=z_rounded[c][:].rearrange("p (j t) -> p j t", t=PACK),
                in0=hidden[c][:].rearrange("p (t j) -> p j t", t=PACK),
                scalar=0.0,
                in1=gain[:].unsqueeze(1).to_broadcast([P, CHUNK, PACK]),
                op0=ALU.max,
                op1=ALU.mult,
            )

        make_z(0)
        w1_wds = tile("w1_wds", N, U32)
        deal_words(nc.gpsimd, w1_wds[:], w1_word_plain[:])

        def quantize_z(c):
            nc.vector.quantize_mx(out=z_words[c][:].bitcast(FP8X4), scales=z_bytes[c][:], in_=z_rounded[c][:])

        def shortcut(c, t, target):
            cols = slice(t * P, (t + 1) * P)
            rhs, rhs_scale = tokens(c)
            nc.tensor.matmul_mx(
                out=target, lhsT=k2_words[:, cols].bitcast(FP8X4), lhsT_scale=k2_bytes[:, cols],
                rhs=rhs, rhs_scale=rhs_scale, start=True, stop=False,
            )

        def dense(c, t, target):
            cols = slice(t * P, (t + 1) * P)
            nc.tensor.matmul_mx(
                out=target, lhsT=w1_wds[:, cols].bitcast(FP8X4), lhsT_scale=w1_bytes[:, cols],
                rhs=z_words[c][:].bitcast(FP8X4), rhs_scale=z_bytes[c][:], start=False, stop=True,
            )

        def store_y(c):
            nc.sync.dma_start(
                out_0.rearrange("(p t) j -> p t j", t=PACK)[:, :, c * CHUNK : (c + 1) * CHUNK],
                y[c][:].rearrange("p (t j) -> p t j", t=PACK),
            )

        def second_layer(c):
            bank = ps.tile([P, PACK * CHUNK], F32, name="result%d" % c)
            for t in range(PACK):
                target = bank[:, t * CHUNK : (t + 1) * CHUNK]
                shortcut(c, t, target)
                dense(c, t, target)
            nc.scalar.activation(out=y[c][:], in_=bank[:], func=COPY, scale=0.0625)
            store_y(c)

        def last_shortcut():
            c = CHUNKS - 1
            tags = ["spare"] + ["hidden%d" % i for i in range(PACK - 1)]
            banks = [ps.tile([P, PACK * CHUNK], F32, name="last%d" % t, tag=tags[t]) for t in range(PACK)]
            for t in range(PACK):
                shortcut(c, t, banks[t][:, :CHUNK])
            return banks

        def last_dense(banks):
            c = CHUNKS - 1
            for t in range(PACK):
                dense(c, t, banks[t][:, :CHUNK])
                part = y[c][:, t * CHUNK : (t + 1) * CHUNK]
                if t % 2:
                    nc.vector.tensor_scalar_mul(part, banks[t][:, :CHUNK], 0.0625)
                else:
                    nc.scalar.activation(out=part, in_=banks[t][:, :CHUNK], func=COPY, scale=0.0625)
            store_y(c)

        def quantize_y(half):
            rounded = tile("y_rounded%d" % half, PACK * HALF, BF16, "z_rounded%d" % (CHUNKS - 1 - half))
            for c in range(2 * half, 2 * half + 2):
                part = rounded[:, (c % 2) * PACK * CHUNK : (c % 2 + 1) * PACK * CHUNK]
                if c == CHUNKS - 2:
                    nc.scalar.copy(
                        out=part.rearrange("p (j t) -> p j t", t=PACK),
                        in_=y[c][:].rearrange("p (t j) -> p j t", t=PACK),
                    )
                else:
                    nc.vector.tensor_copy(
                        out=part.rearrange("p (a i t) -> p a t i", t=PACK, i=PACK),
                        in_=y[c][:].rearrange("p (t a i) -> p a t i", t=PACK, i=PACK),
                    )
            y_words = tile("y_words%d" % half, HALF, U32, "z_words%d" % (CHUNKS - 1 - half))
            cols = slice(half * HALF, (half + 1) * HALF)
            nc.vector.quantize_mx(out=y_words[:].bitcast(FP8X4), scales=y_bytes[:, cols], in_=rounded[:])
            nc.sync.dma_start(words_of(out_1)[:, cols], y_words[:].bitcast(I32))

        for c in range(1, CHUNKS):
            make_z(c)
            quantize_z(c - 1)
            second_layer(c - 1)
        banks = last_shortcut()
        quantize_z(CHUNKS - 1)
        last_dense(banks)
        for half in range(2):
            quantize_y(half)
        y_rows = out_2[0].bitcast(I32)
        for i in range(4):
            queue = nc.sync if i % 2 else nc.scalar
            queue.dma_start(y_rows[i:16:4, :], y_bytes[i:P:32, :].bitcast(I32))
